import numpy as np
import ml_dtypes

BF16 = ml_dtypes.bfloat16


def bf(x):
    return np.asarray(x, np.float32).astype(BF16)


def f32(x):
    return np.asarray(x, np.float32)


def f64(x):
    return np.asarray(x).astype(np.float64)


def striped(idx):
    return np.tile(idx.reshape(-1, 16).T, (8, 1))


def rows(idx, k):
    return np.tile(idx, (k, 1))


def look(tab, idx):
    return np.take_along_axis(f64(tab), rows(idx, len(tab)), axis=1)


K, S, D, V, N, M = 256, 256, 2, 64, 128, 256


def setup_inputs():
    return {"tab": f32(np.random.standard_normal((K, S))), "x0": f32(np.random.standard_normal((K, V))), "w": bf(np.random.standard_normal((K, M)) / np.sqrt(K)), "b": f32(0.5 * np.random.standard_normal((M, 1))), "offs": striped(np.random.permutation(S)[:N])}


def reference(tab, x0, w, b, offs):
    idx = offs[:16].T.reshape(-1)
    x = f64(x0)
    for d in range(D):
        x = np.minimum(x, look(tab, idx[d * V:(d + 1) * V]))
    y = f64(w).T @ x
    return np.maximum(y + f64(b), 0.0)

@@ -1,0 +1,50 @@
+import concourse.mybir as mybir
+
+F32, BF16, U16 = mybir.dt.float32, mybir.dt.bfloat16, mybir.dt.uint16
+MIN = mybir.AluOpType.min
+RELU = mybir.ActivationFunctionType.Relu
+
+P = 128
+K, S, D, V, M = 256, 256, 2, 64, 256
+KB, MB = K // P, M // P
+FLOPS = 2 * K * M * V + D * K * V
+
+
+def tile_lookup_pool_min_relu_kernel(tc, tab, x0, w, b, offs, out):
+    nc = tc.nc
+    with (
+        tc.tile_pool(name="held", bufs=1) as held,
+        tc.psum_pool(name="psum", bufs=1) as psum,
+    ):
+        offsets = held.tile([P, D * V // 16], U16, name="offsets")
+        tables = [held.tile([P, S], F32, name=f"table{k}") for k in range(KB)]
+        centres = held.tile([P, KB, V], F32, name="centres")
+        weights = held.tile([P, KB, M], BF16, name="weights")
+        bias = held.tile([P, MB], F32, name="bias")
+
+        nc.sync.dma_start(offsets[:], offs)
+        nc.scalar.dma_start(tables[0][:], tab[0:P, :])
+        nc.sync.dma_start(centres[:], x0.rearrange("(k p) v -> p k v", p=P))
+        nc.scalar.dma_start(tables[1][:], tab[P : 2 * P, :])
+        nc.sync.dma_start(weights[:], w.rearrange("(k p) m -> p k m", p=P))
+        nc.scalar.dma_start(bias[:], b.rearrange("(m p) one -> p (m one)", p=P))
+
+        sums = [psum.tile([P, V], F32, name=f"sum{m}") for m in range(MB)]
+        for k in range(KB):
+            smallest = centres[:, k, :]
+            for d in range(D):
+                pooled = held.tile([P, V], F32, name=f"pooled{k}_{d}")
+                piece = offsets[:, d * V // 16 : (d + 1) * V // 16]
+                nc.vector.tensor_tensor(pooled[:], tables[k][:].indirect(piece), smallest, MIN)
+                smallest = pooled[:]
+            x = held.tile([P, V], BF16, name=f"x{k}")
+            nc.scalar.copy(x[:], smallest)
+            for m in range(MB):
+                nc.tensor.matmul(
+                    sums[m][:], weights[:, k, m * P : (m + 1) * P], x[:], start=k == 0, stop=k == KB - 1
+                )
+
+        for m in range(MB):
+            result = held.tile([P, V], F32, name=f"result{m}")
+            nc.scalar.activation(result[:], sums[m][:], RELU, bias=bias[:, m : m + 1])
+            nc.sync.dma_start(out[m * P : (m + 1) * P, :], result[:])

@@ -1,8 +1,7 @@
 import concourse.mybir as mybir
 
 F32, BF16, U16 = mybir.dt.float32, mybir.dt.bfloat16, mybir.dt.uint16
-MIN = mybir.AluOpType.min
-RELU = mybir.ActivationFunctionType.Relu
+MIN, ADD, MAX = mybir.AluOpType.min, mybir.AluOpType.add, mybir.AluOpType.max
 
 P = 128
 K, S, D, V, M = 256, 256, 2, 64, 256
@@ -38,7 +37,7 @@ def tile_lookup_pool_min_relu_kernel(tc, tab, x0, w, b, offs, out):
                 nc.vector.tensor_tensor(pooled[:], tables[k][:].indirect(piece), smallest, MIN)
                 smallest = pooled[:]
             x = held.tile([P, V], BF16, name=f"x{k}")
-            nc.scalar.copy(x[:], smallest)
+            nc.vector.tensor_copy(x[:], smallest)
             for m in range(MB):
                 nc.tensor.matmul(
                     sums[m][:], weights[:, k, m * P : (m + 1) * P], x[:], start=k == 0, stop=k == KB - 1
@@ -46,5 +45,5 @@ def tile_lookup_pool_min_relu_kernel(tc, tab, x0, w, b, offs, out):
 
         for m in range(MB):
             result = held.tile([P, V], F32, name=f"result{m}")
-            nc.scalar.activation(result[:], sums[m][:], RELU, bias=bias[:, m : m + 1])
+            nc.vector.tensor_scalar(result[:], sums[m][:], bias[:, m : m + 1], 0.0, ADD, MAX)
             nc.sync.dma_start(out[m * P : (m + 1) * P, :], result[:])

@@ -2,6 +2,7 @@ import concourse.mybir as mybir
 
 F32, BF16, U16 = mybir.dt.float32, mybir.dt.bfloat16, mybir.dt.uint16
 MIN, ADD, MAX = mybir.AluOpType.min, mybir.AluOpType.add, mybir.AluOpType.max
+RELU = mybir.ActivationFunctionType.Relu
 
 P = 128
 K, S, D, V, M = 256, 256, 2, 64, 256
@@ -20,13 +21,15 @@ def tile_lookup_pool_min_relu_kernel(tc, tab, x0, w, b, offs, out):
         centres = held.tile([P, KB, V], F32, name="centres")
         weights = held.tile([P, KB, M], BF16, name="weights")
         bias = held.tile([P, MB], F32, name="bias")
+        result = held.tile([P, MB, V], F32, name="result")
 
+        rows_of_tab = tab.rearrange("(p k) s -> k p s", k=KB)
         nc.sync.dma_start(offsets[:], offs)
-        nc.scalar.dma_start(tables[0][:], tab[0:P, :])
-        nc.sync.dma_start(centres[:], x0.rearrange("(k p) v -> p k v", p=P))
-        nc.scalar.dma_start(tables[1][:], tab[P : 2 * P, :])
-        nc.sync.dma_start(weights[:], w.rearrange("(k p) m -> p k m", p=P))
-        nc.scalar.dma_start(bias[:], b.rearrange("(m p) one -> p (m one)", p=P))
+        nc.scalar.dma_start(tables[0][:], rows_of_tab[0])
+        nc.sync.dma_start(centres[:], x0.rearrange("(p k) v -> p k v", k=KB))
+        nc.scalar.dma_start(tables[1][:], rows_of_tab[1])
+        nc.sync.dma_start(weights[:], w.rearrange("(p k) m -> p k m", k=KB))
+        nc.scalar.dma_start(bias[:], b.rearrange("(p m) one -> p (m one)", m=MB))
 
         sums = [psum.tile([P, V], F32, name=f"sum{m}") for m in range(MB)]
         for k in range(KB):
@@ -37,13 +40,13 @@ def tile_lookup_pool_min_relu_kernel(tc, tab, x0, w, b, offs, out):
                 nc.vector.tensor_tensor(pooled[:], tables[k][:].indirect(piece), smallest, MIN)
                 smallest = pooled[:]
             x = held.tile([P, V], BF16, name=f"x{k}")
-            nc.vector.tensor_copy(x[:], smallest)
+            if k == 0:
+                nc.scalar.copy(x[:], smallest)
+            else:
+                nc.vector.tensor_copy(x[:], smallest)
             for m in range(MB):
-                nc.tensor.matmul(
-                    sums[m][:], weights[:, k, m * P : (m + 1) * P], x[:], start=k == 0, stop=k == KB - 1
-                )
+                nc.tensor.matmul(sums[m][:], weights[:, k, m::MB], x[:], start=k == 0, stop=k == KB - 1)
 
-        for m in range(MB):
-            result = held.tile([P, V], F32, name=f"result{m}")
-            nc.vector.tensor_scalar(result[:], sums[m][:], bias[:, m : m + 1], 0.0, ADD, MAX)
-            nc.sync.dma_start(out[m * P : (m + 1) * P, :], result[:])
+        nc.scalar.activation(result[:, 0, :], sums[0][:], RELU, bias=bias[:, 0:1])
+        nc.vector.tensor_scalar(result[:, 1, :], sums[1][:], bias[:, 1:2], 0.0, ADD, MAX)
+        nc.sync.dma_start(out.rearrange("(p m) v -> p m v", m=MB), result[:])

@@ -28,8 +28,8 @@ def tile_lookup_pool_min_relu_kernel(tc, tab, x0, w, b, offs, out):
         nc.scalar.dma_start(tables[0][:], rows_of_tab[0])
         nc.sync.dma_start(centres[:], x0.rearrange("(p k) v -> p k v", k=KB))
         nc.scalar.dma_start(tables[1][:], rows_of_tab[1])
-        nc.sync.dma_start(weights[:], w.rearrange("(p k) m -> p k m", k=KB))
-        nc.scalar.dma_start(bias[:], b.rearrange("(p m) one -> p (m one)", m=MB))
+        nc.scalar.dma_start(weights[:], w.rearrange("(p k) m -> p k m", k=KB))
+        nc.sync.dma_start(bias[:], b.rearrange("(p m) one -> p (m one)", m=MB))
 
         sums = [psum.tile([P, V], F32, name=f"sum{m}") for m in range(MB)]
         for k in range(KB):

import concourse.mybir as mybir

F32, BF16, U16 = mybir.dt.float32, mybir.dt.bfloat16, mybir.dt.uint16
MIN, ADD, MAX = mybir.AluOpType.min, mybir.AluOpType.add, mybir.AluOpType.max
RELU = mybir.ActivationFunctionType.Relu

P = 128
K, S, D, V, M = 256, 256, 2, 64, 256
KB, MB = K // P, M // P
FLOPS = 2 * K * M * V + D * K * V


def tile_lookup_pool_min_relu_kernel(tc, tab, x0, w, b, offs, out):
    nc = tc.nc
    with (
        tc.tile_pool(name="held", bufs=1) as held,
        tc.psum_pool(name="psum", bufs=1) as psum,
    ):
        offsets = held.tile([P, D * V // 16], U16, name="offsets")
        tables = [held.tile([P, S], F32, name=f"table{k}") for k in range(KB)]
        centres = held.tile([P, KB, V], F32, name="centres")
        weights = held.tile([P, KB, M], BF16, name="weights")
        bias = held.tile([P, MB], F32, name="bias")
        result = held.tile([P, MB, V], F32, name="result")

        rows_of_tab = tab.rearrange("(p k) s -> k p s", k=KB)
        nc.sync.dma_start(offsets[:], offs)
        nc.scalar.dma_start(tables[0][:], rows_of_tab[0])
        nc.sync.dma_start(centres[:], x0.rearrange("(p k) v -> p k v", k=KB))
        nc.scalar.dma_start(tables[1][:], rows_of_tab[1])
        nc.scalar.dma_start(weights[:], w.rearrange("(p k) m -> p k m", k=KB))
        nc.sync.dma_start(bias[:], b.rearrange("(p m) one -> p (m one)", m=MB))

        sums = [psum.tile([P, V], F32, name=f"sum{m}") for m in range(MB)]
        for k in range(KB):
            smallest = centres[:, k, :]
            for d in range(D):
                pooled = held.tile([P, V], F32, name=f"pooled{k}_{d}")
                piece = offsets[:, d * V // 16 : (d + 1) * V // 16]
                nc.vector.tensor_tensor(pooled[:], tables[k][:].indirect(piece), smallest, MIN)
                smallest = pooled[:]
            x = held.tile([P, V], BF16, name=f"x{k}")
            if k == 0:
                nc.scalar.copy(x[:], smallest)
            else:
                nc.vector.tensor_copy(x[:], smallest)
            for m in range(MB):
                nc.tensor.matmul(sums[m][:], weights[:, k, m::MB], x[:], start=k == 0, stop=k == KB - 1)

        nc.scalar.activation(result[:, 0, :], sums[0][:], RELU, bias=bias[:, 0:1])
        nc.vector.tensor_scalar(result[:, 1, :], sums[1][:], bias[:, 1:2], 0.0, ADD, MAX)
        nc.sync.dma_start(out.rearrange("(p m) v -> p m v", m=MB), result[:])
